import numpy as np, ml_dtypes
CORES = [66,74,82,90,194,202,210,218]
N = 8
import mx_ref
BF = ml_dtypes.bfloat16
def entries(a):
    return np.ascontiguousarray(a.T).reshape(-1)
def table(e):
    return np.ascontiguousarray(np.reshape(e, (-1, 16)).T).astype(np.int32)
def cols(t, e):
    v = np.concatenate([t.reshape(128, -1, 4), np.zeros((128, 1, 4), BF)], axis=1)
    return np.ascontiguousarray(v[:, e]).reshape(128, -1)
def f(rng, *shape):
    return mx_ref.flush((rng.standard_normal(shape, dtype=np.float32) * np.exp2(rng.integers(-2, 3, shape[:-1] + (1,)))).astype(BF))
def wide(rng, *shape, cols=0):
    v = rng.standard_normal(shape, dtype=np.float32) * np.exp2(rng.integers(-12, 13, shape)).astype(np.float32)
    if cols: v *= np.repeat(np.exp2(rng.integers(-cols, cols + 1, shape[:-2] + (1, shape[-1] // 4))) * (rng.random(shape[:-2] + (1, shape[-1] // 4)) > 0.0625), 4, axis=-1).astype(np.float32)
    return mx_ref.flush(v.astype(BF))
T, B, NB, SUM = 512, 256, 3, 768
SIDE = np.array([0 if c < 128 else 1 for c in CORES])
CAP = np.where(SIDE[:, None] == SIDE[None, :], 96, 96)
ST = np.cumsum(CAP, axis=1) - CAP
def lists(rng, alone=False, same=False, full=False, last=False):
    it, it2, ob, bag = np.full((N, SUM), -1), np.full((N, SUM), -1), np.full((N, SUM), -1), np.full((N, SUM), -1)
    one = rng.integers(0, T, N)
    none = rng.permutation(N) if alone else np.full(N, -1)
    for r in range(N):
        has = np.zeros((N, B), bool)
        free = np.where(np.arange(N) == none[r], 0, CAP[:, r])
        if full: has[:, rng.integers(0, B)] = True
        g = np.flatnonzero(~has.any(axis=0))
        has[rng.permutation(np.repeat(np.arange(N), free - has.sum(axis=1)))[:len(g)], g] = True
        for s in range(N):
            n = CAP[s, r]; h = has[s].sum()
            k = n if full else rng.integers(h, free[s] + 1)
            has[s, rng.permutation(np.flatnonzero(~has[s]))[:k - h]] = True
            j = np.flatnonzero(has[s]); c = rng.permutation(n)[:k]
            if last: j, c = j[::-1], np.sort(c)
            else: j = rng.permutation(j)
            u = np.full(k, one[s]) if same else rng.integers(0, T, k)
            v = (u + rng.integers(1, T, k)) % T if same else rng.integers(0, T, k)
            v = np.where(rng.random(k) < (1.0 if alone else 0.25), -1, v)
            it[s, ST[s, r] + c] = u; it2[s, ST[s, r] + c] = v; ob[s, ST[s, r] + c] = j; bag[r, ST[r, s] + c] = j
    return {"it": np.stack([table(e) for e in it]), "it2": np.stack([table(e) for e in it2]), "ob": np.stack([table(e) for e in ob]), "bag": np.stack([table(e) for e in bag])}
def setup_inputs(rng):
    return {"ex": f(rng, N, 128, 4 * T), "w": f(rng, N, 128, 512 * NB), **lists(rng)}
def setup_inputs_alone(rng):
    return {**setup_inputs(rng), **lists(rng, alone=True)}
def setup_inputs_full(rng):
    return {**setup_inputs(rng), **lists(rng, full=True)}
def setup_inputs_last(rng):
    return {**setup_inputs(rng), **lists(rng, last=True)}
def setup_inputs_same(rng):
    return {**setup_inputs(rng), **lists(rng, same=True)}
def setup_inputs_spread(rng):
    d = setup_inputs(rng); d["ex"] = wide(rng, N, 128, 4 * T, cols=6); return d
def check_inputs(d):
    b = []
    it, it2, ob, bag = [np.stack([entries(d[k][r]) for r in range(N)]) for k in ("it", "it2", "ob", "bag")]
    if it.min() < -1 or it.max() >= T: b.append("it")
    if it2.min() < -1 or it2.max() >= T: b.append("it2")
    if (it2[it < 0] != -1).any(): b.append("a second item in an empty slot")
    if ob.min() < -1 or ob.max() >= B: b.append("ob")
    if bag.min() < -1 or bag.max() >= B: b.append("bag")
    for r in range(N):
        for s in range(N):
            n = CAP[s, r]; u = it[s, ST[s, r]:ST[s, r] + n]; j = bag[r, ST[r, s]:ST[r, s] + n]
            if ((u < 0) != (j < 0)).any(): b.append("bag and it differ in their empty slots")
            if (ob[s, ST[s, r]:ST[s, r] + n] != j).any(): b.append("ob and bag differ")
            j = j[j >= 0]
            if len(set(j.tolist())) != len(j): b.append("a bag named twice")
        if not set(range(B)) <= set(bag[r].tolist()): b.append("a bag without parts")
    return b
def reference(ex, w, it, it2, ob, bag):
    y = np.zeros((N, 128, B * NB), np.float32)
    for r in range(N):
        W = [mx_ref.quantize(w[r][:, 512 * o:512 * o + 512]) for o in range(NB)]
        for s in range(N):
            n = CAP[s, r]
            u, v = entries(it[s])[ST[s, r]:ST[s, r] + n], entries(it2[s])[ST[s, r]:ST[s, r] + n]
            part = (cols(ex[s], u).astype(np.float32) + cols(ex[s], v).astype(np.float32)).astype(BF)
            P = mx_ref.quantize(part)
            j = entries(bag[r])[ST[r, s]:ST[r, s] + n]; used = j >= 0
            for o in range(NB): y[r][:, B * o + j[used]] += mx_ref.matmul(W[o], P)[:, used]
    return {"y": y}

@@ -1,0 +1,248 @@
+from concourse.bass import DstId, RemoteDMATransfer
+from concourse.mybir import dt, AluOpType, ActivationFunctionType
+
+N, CAP, BAGS, NB, ITEMS = 8, 96, 256, 3, 512
+PAIR = 2 * CAP
+LC = CAP // 16
+LIST = N * LC
+ZERO = 16
+WIN = ZERO + 4 * ITEMS
+INV = 464
+ZW = 200
+NCH = 4
+F32, BF, I32, U16 = "float32", "bfloat16", "int32", "uint16"
+SCRATCH = {
+    "exw": ("sbuf", [128, WIN], BF),
+    "wt": ("sbuf", [128, 512 * NB], BF),
+    "wq": ("sbuf", [128, 128 * NB], "float8_e4m3fn_x4"),
+    "wsc": ("sbuf", [128, 128 * NB], "uint8"),
+    "lraw": ("sbuf", [128, 2 * LIST], I32),
+    "hu": ("sbuf", [128, 4 * N * CAP], BF),
+    "h": ("sbuf", [128, 4 * N * CAP], BF),
+    "q": ("sbuf", [128, N * CAP], "float8_e4m3fn_x4"),
+    "qsc": ("sbuf", [128, N * CAP], "uint8"),
+    "lq": ("sbuf", [128, N * CAP], "float8_e4m3fn_x4"),
+    "lsc": ("sbuf", [128, N * CAP], "uint8"),
+    "bagg": ("sbuf", [128, LC], I32),
+    "neg": ("sbuf", [128, LC], I32),
+    "dumpo": ("sbuf", [128, LC], I32),
+    "dmp": ("sbuf", [128, LC], I32),
+    "bo": ("sbuf", [128, LC], I32),
+    "boff": ("sbuf", [128, LC], U16),
+    "ip": ("sbuf", [128, 1], I32),
+    "ip2": ("sbuf", [128, 1], I32),
+    "ipf": ("sbuf", [128, 1], F32),
+    "io1": ("sbuf", [128, CAP], F32),
+    "vals": ("sbuf", [128, CAP], F32),
+    "inv": ("sbuf", [128, INV], F32),
+    "invt": ("sbuf", [128, BAGS], F32),
+    "cc": ("sbuf", [128, 16], F32),
+    "raw": ("sbuf", [32, 128], F32),
+    "offb": ("sbuf", [128, 128], U16),
+    "acc": ("sbuf", [128, NB * BAGS], F32),
+    "ps": ("psum", [128, 4096], F32),
+}
+for _t in range(4):
+    SCRATCH["off%d" % _t] = ("sbuf", [128, 2 * LIST], U16)
+for _k in range(NCH + 1):
+    SCRATCH["z%d" % _k] = ("sbuf", [128, NB * ZW], F32)
+SEMAPHORES = ["ldl", "ldx", "ldb", "ldw", "ldr", "vs", "ss", "ps", "gs", "loc", "st", "a0", "a1", "a2", "a3"]
+
+
+def rank_program(g, core, T, topo):
+    r = T.rank_of(core)
+    if r is None:
+        return
+    Alu, Copy = AluOpType, ActivationFunctionType.Copy
+    pair, mem = r // 2, r % 2
+    order = sorted(range(1, NCH), key=lambda x: (topo.host(T.cores[2 * x]) == topo.host(T.cores[0]), -x)) + [0]
+
+    cnt = {"vs": 0, "ss": 0, "ps": 0, "gs": 0}
+    seen = {}
+    queues = {"v": g.vector, "s": g.scalar, "t": g.tensor, "y": g.sync, "g": g}
+
+    def need(qn, sem, val):
+        if val > seen.get((qn, sem), 0):
+            queues[qn].wait_ge(T.sem[sem], val)
+            seen[(qn, sem)] = val
+
+    def did(sem, ins):
+        ins.then_inc(T.sem[sem], 1)
+        cnt[sem] += 1
+        return cnt[sem]
+
+    for grp in range(2):
+        g.sync.dma_start(T.lraw[16 * grp:16 * grp + 16, 0:LIST], T["it"][:, :]).then_inc(T.sem.ldl, 16)
+        g.scalar.dma_start(T.lraw[16 * grp:16 * grp + 16, LIST:2 * LIST], T["it2"][:, :]).then_inc(T.sem.ldl, 16)
+    g.sync.dma_start(T.exw[:, ZERO:WIN], T.ex[:, :]).then_inc(T.sem.ldx, 16)
+    for s in range(N):
+        q = g.scalar if s % 2 else g.sync
+        q.dma_start(T.bagg[16 * s:16 * s + 16, :], T.bag[:, LC * s:LC * s + LC]).then_inc(T.sem.ldb, 16)
+    g.sync.dma_start(T.wt[:, :], T.w[:, :]).then_inc(T.sem.ldw, 16)
+
+    did("gs", g.iota(T.ip[:, :], [[1, 1]], 0, 1))
+    did("gs", g.iota(T.dumpo[:, :], [[16, LC]], BAGS + 1, 1))
+    g_io = did("gs", g.iota(T.io1[:, :], [[1, CAP]], 1, 0, allow_small_or_imprecise_dtypes=True))
+    did("vs", g.vector.memset(T.exw[:, 0:ZERO], 0.0))
+    did("vs", g.vector.memset(T.inv[:, :], 0.0))
+    for k in range(NCH + 1):
+        if k >= NCH - 1:
+            v_z = did("vs", g.vector.memset(T["z%d" % k][:, :], 0.0))
+        else:
+            for o in range(NB):
+                v_z = did("vs", g.vector.memset(T["z%d" % k][:, o * ZW:o * ZW + 1], 0.0))
+    need("v", "gs", g_io)
+    k = did("vs", g.vector.tensor_scalar(T.ip2[:, :], T.ip[:, :], 4, 1, Alu.arith_shift_right, Alu.bitwise_and))
+    need("v", "vs", k)
+    k = did("vs", g.vector.tensor_scalar(T.ipf[:, :], T.ip2[:, :], float(CAP), None, Alu.mult))
+    need("v", "vs", k)
+    v_vals = did("vs", g.vector.tensor_scalar(T.vals[:, :], T.io1[:, :], T.ipf[:, 0:1], None, Alu.add))
+
+    need("v", "ldl", 64)
+    for qd in range(1, 4):
+        k = did("vs", g.vector.tensor_copy(T.lraw[32 * qd:32 * qd + 32, :], T.lraw[0:32, :]))
+    need("v", "vs", k)
+    v_off = []
+    for t in range(4):
+        v_off.append(did("vs", g.vector.tensor_scalar(T["off%d" % t][:, :], T.lraw[:, :], 4.0, float(ZERO + t), Alu.mult, Alu.add)))
+
+    need("v", "ldb", 16 * N)
+    k = did("vs", g.vector.tensor_scalar(T.neg[:, :], T.bagg[:, :], 0, None, Alu.is_lt))
+    need("v", "vs", k)
+    k = did("vs", g.vector.tensor_tensor(T.dmp[:, :], T.neg[:, :], T.dumpo[:, :], Alu.mult))
+    need("v", "vs", k)
+    k = did("vs", g.vector.tensor_tensor(T.bo[:, :], T.bagg[:, :], T.dmp[:, :], Alu.add))
+    need("v", "vs", k)
+    k = did("vs", g.vector.tensor_copy(T.boff[:, :], T.bo[:, :]))
+    need("v", "vs", k)
+    k = did("vs", g.vector.tensor_copy(T.inv[:, 0:INV].indirect(T.boff[:, 0:LC]), T.vals[:, :]))
+    need("v", "vs", k)
+    k = did("vs", g.vector.transpose(T.invt[:, :], T.inv[:, 0:BAGS]))
+    need("v", "vs", k)
+    did("vs", g.vector.tensor_copy(T.cc[:, 0:8], T.invt[:, 0:BAGS:32]))
+    v_cc = did("vs", g.vector.tensor_copy(T.cc[:, 8:16], T.invt[:, 16:BAGS:32]))
+    need("y", "vs", v_cc)
+    for grp in range(2):
+        for a in range(4):
+            for hh in range(2):
+                g.sync.dma_start(T.raw[16 * grp:16 * grp + 16, 64 * hh + 16 * a:64 * hh + 16 * a + 16],
+                                 T.cc[32 * a + 16 * hh:32 * a + 16 * hh + 16, :]).then_inc(T.sem.ldr, 16)
+
+    s_u = {}
+    need("s", "ldx", 16)
+    for c, x in enumerate(order):
+        l0 = 2 * LC * (pair ^ x)
+        for t in range(4):
+            need("s", "vs", v_off[t])
+            b = (4 * c + t) * PAIR
+            s_u[c, t] = did("ss", g.scalar.activation(T.hu[:, b:b + PAIR], T.exw[:, 0:WIN].indirect(T["off%d" % t][:, l0:l0 + 2 * LC]), Copy))
+    need("v", "ldx", 16)
+    v_q = []
+    for c, x in enumerate(order):
+        l0 = LIST + 2 * LC * (pair ^ x)
+        for t in range(4):
+            need("v", "vs", v_off[t])
+            need("v", "ss", s_u[c, t])
+            b = (4 * c + t) * PAIR
+            k = did("vs", g.vector.tensor_tensor(T.h[:, 4 * c * PAIR + t:4 * (c + 1) * PAIR:4],
+                                                 T.exw[:, 0:WIN].indirect(T["off%d" % t][:, l0:l0 + 2 * LC]), T.hu[:, b:b + PAIR], Alu.add))
+        need("v", "vs", k)
+        v_q.append(did("vs", g.vector.quantize_mx(T.q[:, c * PAIR:(c + 1) * PAIR], T.qsc[:, c * PAIR:(c + 1) * PAIR],
+                                                  T.h[:, 4 * c * PAIR:4 * (c + 1) * PAIR])))
+
+    def land(c, rx_mem, tx_mem):
+        if c < 2:
+            return c * PAIR + CAP * tx_mem
+        base = 2 * PAIR
+        if c == 2:
+            return base + CAP * tx_mem + (0 if rx_mem == 0 else CAP)
+        return base + (PAIR if rx_mem == 0 else 0)
+
+    loc = 0
+    arr = []
+    for c, x in enumerate(order):
+        dests = [2 * (pair ^ x) + m for m in range(2) if 2 * (pair ^ x) + m != r]
+        need("g", "vs", v_q[c])
+        for kind in range(2):
+            tr, tot = [], 0
+            for i, d in enumerate(dests):
+                dst = T.cores[d]
+                eng = topo.engines(core, dst)
+                n = len(eng) // len(dests)
+                rid, pnc = topo.addr(dst, core)
+                a = c * PAIR + CAP * (d % 2)
+                b = land(c, d % 2, mem)
+                if kind == 0:
+                    src, out = T.q[:, a:a + CAP].bitcast(dt.uint8), T.lq[:, b:b + CAP].bitcast(dt.uint8)
+                else:
+                    src, out = T.qsc[:, a:a + CAP], T.lsc[:, b:b + CAP]
+                tr.append(RemoteDMATransfer(dst_ids=[DstId(rid=rid, pnc=pnc)], dma_engine_mask=sum(1 << e for e in eng[i * n:(i + 1) * n]),
+                                            remote_sem=T.sem["a%d" % c], src=src, dst=out))
+                tot += n
+            g.remote_dma_fused(tr, local_sem=T.sem.loc)
+            loc += tot
+        arr.append(2 * tot)
+
+    need("v", "ldw", 16)
+    v_w = did("vs", g.vector.quantize_mx(T.wq[:, :], T.wsc[:, :], T.wt[:, :]))
+    need("v", "ldr", 16 * 16)
+    for hh in range(2):
+        for qd in range(4):
+            v_ob = did("vs", g.vector.tensor_copy(T.offb[32 * qd:32 * qd + 32, hh:128:2], T.raw[0:32, 64 * hh:64 * hh + 64]))
+
+    need("s", "vs", v_z)
+    need("t", "vs", v_w)
+    use = 0
+    bank_free = [0] * 8
+    a_v, s_own = [0] * NB, [0] * NB
+    for stage in range(NCH + 1):
+        z = T["z%d" % (NCH if stage == 0 else stage - 1)]
+        if stage == 0:
+            first = (NCH - 1) * PAIR
+            owners, src, ssc, lo, width = [r], T.q, T.qsc, CAP * mem, CAP
+            need("t", "vs", v_q[NCH - 1])
+        else:
+            c = stage - 1
+            src, ssc = T.lq, T.lsc
+            owners = [2 * (pair ^ order[c]) + m for m in range(2)]
+            lo, width = 0, PAIR
+            first = c * PAIR
+            if c == 2:
+                first = land(2, mem, 0)
+            if c == 3:
+                owners = [r ^ 1]
+                tx = 1 - mem
+                first = land(3, mem, tx) - CAP * tx
+                lo, width = CAP * tx, CAP
+            need("t", "a%d" % c, arr[c])
+        zs = []
+        for o in range(NB):
+            bk = use % 8
+            use += 1
+            need("t", "ss", bank_free[bk])
+            p = did("ps", g.tensor.matmul_mx(T.ps[:, 512 * bk:512 * bk + PAIR], T.wq[:, 128 * o:128 * o + 128], T.wsc[:, 128 * o:128 * o + 128],
+                                             src[:, first:first + PAIR], ssc[:, first:first + PAIR], True, True))
+            need("s", "ps", p)
+            bank_free[bk] = did("ss", g.scalar.activation(z[:, o * ZW + 1 + lo:o * ZW + 1 + lo + width],
+                                                          T.ps[:, 512 * bk + lo:512 * bk + lo + width], Copy))
+            zs.append(bank_free[bk])
+        need("s", "vs", v_ob)
+        for s in owners:
+            for o in range(NB):
+                y = T.acc[:, BAGS * o:BAGS * (o + 1)]
+                win = z[:, o * ZW:o * ZW + 1 + lo + width].indirect(T.offb[:, 16 * s:16 * s + 16])
+                if stage == 0:
+                    need("s", "ss", zs[o])
+                    s_own[o] = did("ss", g.scalar.activation(y, win, Copy))
+                else:
+                    need("v", "ss", max(zs[o], s_own[o]))
+                    need("v", "vs", a_v[o])
+                    a_v[o] = did("vs", g.vector.tensor_tensor(y, win, y, Alu.add))
+                if stage == NCH:
+                    need("y", "vs", a_v[o])
+                    g.sync.dma_start(T.y[:, BAGS * o:BAGS * (o + 1)], y).then_inc(T.sem.st, 16)
+
+    need("g", "loc", loc)
+    for sem in ("gs", "vs", "ss", "ps"):
+        need("g", sem, cnt[sem])
+    need("g", "st", 16 * NB)

@@ -10,6 +10,7 @@ WIN = ZERO + 4 * ITEMS
 INV = 464
 ZW = 200
 NCH = 4
+OWN = 2
 F32, BF, I32, U16 = "float32", "bfloat16", "int32", "uint16"
 SCRATCH = {
     "exw": ("sbuf", [128, WIN], BF),
@@ -55,7 +56,8 @@ def rank_program(g, core, T, topo):
         return
     Alu, Copy = AluOpType, ActivationFunctionType.Copy
     pair, mem = r // 2, r % 2
-    order = sorted(range(1, NCH), key=lambda x: (topo.host(T.cores[2 * x]) == topo.host(T.cores[0]), -x)) + [0]
+    order = sorted(range(1, NCH), key=lambda x: (topo.host(T.cores[2 * x]) == topo.host(T.cores[0]), -x))
+    order.insert(OWN, 0)
 
     cnt = {"vs": 0, "ss": 0, "ps": 0, "gs": 0}
     seen = {}
@@ -74,29 +76,28 @@ def rank_program(g, core, T, topo):
     for grp in range(2):
         g.sync.dma_start(T.lraw[16 * grp:16 * grp + 16, 0:LIST], T["it"][:, :]).then_inc(T.sem.ldl, 16)
         g.scalar.dma_start(T.lraw[16 * grp:16 * grp + 16, LIST:2 * LIST], T["it2"][:, :]).then_inc(T.sem.ldl, 16)
-    g.sync.dma_start(T.exw[:, ZERO:WIN], T.ex[:, :]).then_inc(T.sem.ldx, 16)
     for s in range(N):
         q = g.scalar if s % 2 else g.sync
         q.dma_start(T.bagg[16 * s:16 * s + 16, :], T.bag[:, LC * s:LC * s + LC]).then_inc(T.sem.ldb, 16)
+    g.sync.dma_start(T.exw[:, ZERO:WIN], T.ex[:, :]).then_inc(T.sem.ldx, 16)
     g.sync.dma_start(T.wt[:, :], T.w[:, :]).then_inc(T.sem.ldw, 16)
 
     did("gs", g.iota(T.ip[:, :], [[1, 1]], 0, 1))
     did("gs", g.iota(T.dumpo[:, :], [[16, LC]], BAGS + 1, 1))
     g_io = did("gs", g.iota(T.io1[:, :], [[1, CAP]], 1, 0, allow_small_or_imprecise_dtypes=True))
+    for k in range(NCH + 1):
+        whole = k in (OWN, NCH)
+        for o in range(1 if whole else NB):
+            n = NB * ZW if whole else 1
+            g_z = did("gs", g.iota(T["z%d" % k][:, o * ZW:o * ZW + n], [[0, n]], 0, 0, allow_small_or_imprecise_dtypes=True))
     did("vs", g.vector.memset(T.exw[:, 0:ZERO], 0.0))
     did("vs", g.vector.memset(T.inv[:, :], 0.0))
-    for k in range(NCH + 1):
-        if k >= NCH - 1:
-            v_z = did("vs", g.vector.memset(T["z%d" % k][:, :], 0.0))
-        else:
-            for o in range(NB):
-                v_z = did("vs", g.vector.memset(T["z%d" % k][:, o * ZW:o * ZW + 1], 0.0))
     need("v", "gs", g_io)
     k = did("vs", g.vector.tensor_scalar(T.ip2[:, :], T.ip[:, :], 4, 1, Alu.arith_shift_right, Alu.bitwise_and))
     need("v", "vs", k)
     k = did("vs", g.vector.tensor_scalar(T.ipf[:, :], T.ip2[:, :], float(CAP), None, Alu.mult))
     need("v", "vs", k)
-    v_vals = did("vs", g.vector.tensor_scalar(T.vals[:, :], T.io1[:, :], T.ipf[:, 0:1], None, Alu.add))
+    did("vs", g.vector.tensor_scalar(T.vals[:, :], T.io1[:, :], T.ipf[:, 0:1], None, Alu.add))
 
     need("v", "ldl", 64)
     for qd in range(1, 4):
@@ -149,14 +150,23 @@ def rank_program(g, core, T, topo):
         need("v", "vs", k)
         v_q.append(did("vs", g.vector.quantize_mx(T.q[:, c * PAIR:(c + 1) * PAIR], T.qsc[:, c * PAIR:(c + 1) * PAIR],
                                                   T.h[:, 4 * c * PAIR:4 * (c + 1) * PAIR])))
+        if c == OWN - 1:
+            need("v", "ldw", 16)
+            v_w = did("vs", g.vector.quantize_mx(T.wq[:, :], T.wsc[:, :], T.wt[:, :]))
+        if c == OWN:
+            need("v", "ldr", 16 * 16)
+            for hh in range(2):
+                k = did("vs", g.vector.tensor_copy(T.offb[0:32, hh:128:2], T.raw[:, 64 * hh:64 * hh + 64]))
+            need("v", "vs", k)
+            for qd in range(1, 4):
+                v_ob = did("vs", g.vector.tensor_copy(T.offb[32 * qd:32 * qd + 32, :], T.offb[0:32, :]))
 
     def land(c, rx_mem, tx_mem):
-        if c < 2:
-            return c * PAIR + CAP * tx_mem
-        base = 2 * PAIR
-        if c == 2:
-            return base + CAP * tx_mem + (0 if rx_mem == 0 else CAP)
-        return base + (PAIR if rx_mem == 0 else 0)
+        if c == 1:
+            return PAIR + CAP * tx_mem + (0 if rx_mem == 0 else CAP)
+        if c == OWN:
+            return PAIR + (PAIR if rx_mem == 0 else 0)
+        return (0 if c == 0 else PAIR + PAIR + CAP) + CAP * tx_mem
 
     loc = 0
     arr = []
@@ -183,38 +193,29 @@ def rank_program(g, core, T, topo):
             loc += tot
         arr.append(2 * tot)
 
-    need("v", "ldw", 16)
-    v_w = did("vs", g.vector.quantize_mx(T.wq[:, :], T.wsc[:, :], T.wt[:, :]))
-    need("v", "ldr", 16 * 16)
-    for hh in range(2):
-        for qd in range(4):
-            v_ob = did("vs", g.vector.tensor_copy(T.offb[32 * qd:32 * qd + 32, hh:128:2], T.raw[0:32, 64 * hh:64 * hh + 64]))
-
-    need("s", "vs", v_z)
+    need("s", "gs", g_z)
     need("t", "vs", v_w)
     use = 0
     bank_free = [0] * 8
-    a_v, s_own = [0] * NB, [0] * NB
-    for stage in range(NCH + 1):
-        z = T["z%d" % (NCH if stage == 0 else stage - 1)]
-        if stage == 0:
-            first = (NCH - 1) * PAIR
+    a_v, s_base = [0] * NB, [0] * NB
+    own_win, z_own = [], []
+    for stage in (NCH, 0, 1, OWN, NCH - 1):
+        z = T["z%d" % stage]
+        src, ssc = T.lq, T.lsc
+        lo, width = 0, PAIR
+        if stage == NCH:
+            first = OWN * PAIR
             owners, src, ssc, lo, width = [r], T.q, T.qsc, CAP * mem, CAP
-            need("t", "vs", v_q[NCH - 1])
+            need("t", "vs", v_q[OWN])
+        elif stage == OWN:
+            owners = [r ^ 1]
+            lo, width = CAP * (1 - mem), CAP
+            first = land(OWN, mem, 1 - mem) - lo
         else:
-            c = stage - 1
-            src, ssc = T.lq, T.lsc
-            owners = [2 * (pair ^ order[c]) + m for m in range(2)]
-            lo, width = 0, PAIR
-            first = c * PAIR
-            if c == 2:
-                first = land(2, mem, 0)
-            if c == 3:
-                owners = [r ^ 1]
-                tx = 1 - mem
-                first = land(3, mem, tx) - CAP * tx
-                lo, width = CAP * tx, CAP
-            need("t", "a%d" % c, arr[c])
+            owners = [2 * (pair ^ order[stage]) + m for m in range(2)]
+            first = land(stage, mem, 0)
+        if stage < NCH:
+            need("t", "a%d" % stage, arr[stage])
         zs = []
         for o in range(NB):
             bk = use % 8
@@ -222,25 +223,28 @@ def rank_program(g, core, T, topo):
             need("t", "ss", bank_free[bk])
             p = did("ps", g.tensor.matmul_mx(T.ps[:, 512 * bk:512 * bk + PAIR], T.wq[:, 128 * o:128 * o + 128], T.wsc[:, 128 * o:128 * o + 128],
                                              src[:, first:first + PAIR], ssc[:, first:first + PAIR], True, True))
+            if stage == 0:
+                need("s", "vs", v_ob)
+                need("s", "ss", z_own[o])
+                s_base[o] = did("ss", g.scalar.activation(T.acc[:, BAGS * o:BAGS * (o + 1)], own_win[o], Copy))
             need("s", "ps", p)
-            bank_free[bk] = did("ss", g.scalar.activation(z[:, o * ZW + 1 + lo:o * ZW + 1 + lo + width],
-                                                          T.ps[:, 512 * bk + lo:512 * bk + lo + width], Copy))
-            zs.append(bank_free[bk])
-        need("s", "vs", v_ob)
-        for s in owners:
-            for o in range(NB):
-                y = T.acc[:, BAGS * o:BAGS * (o + 1)]
-                win = z[:, o * ZW:o * ZW + 1 + lo + width].indirect(T.offb[:, 16 * s:16 * s + 16])
-                if stage == 0:
-                    need("s", "ss", zs[o])
-                    s_own[o] = did("ss", g.scalar.activation(y, win, Copy))
-                else:
-                    need("v", "ss", max(zs[o], s_own[o]))
-                    need("v", "vs", a_v[o])
-                    a_v[o] = did("vs", g.vector.tensor_tensor(y, win, y, Alu.add))
-                if stage == NCH:
-                    need("y", "vs", a_v[o])
-                    g.sync.dma_start(T.y[:, BAGS * o:BAGS * (o + 1)], y).then_inc(T.sem.st, 16)
+            zs.append(did("ss", g.scalar.activation(z[:, o * ZW + 1 + lo:o * ZW + 1 + lo + width],
+                                                    T.ps[:, 512 * bk + lo:512 * bk + lo + width], Copy)))
+            bank_free[bk] = zs[o]
+        last = stage == NCH - 1
+        for s, o in [(s, o) for o in range(NB) for s in owners] if last else [(s, o) for s in owners for o in range(NB)]:
+            y = T.acc[:, BAGS * o:BAGS * (o + 1)]
+            win = z[:, o * ZW:o * ZW + 1 + lo + width].indirect(T.offb[:, 16 * s:16 * s + 16])
+            if stage == NCH:
+                own_win.append(win)
+                z_own.append(zs[o])
+                continue
+            need("v", "ss", max(zs[o], s_base[o]))
+            need("v", "vs", a_v[o])
+            a_v[o] = did("vs", g.vector.tensor_tensor(y, win, y, Alu.add))
+            if last and s == owners[-1]:
+                need("y", "vs", a_v[o])
+                g.sync.dma_start(T.y[:, BAGS * o:BAGS * (o + 1)], y).then_inc(T.sem.st, 16)
 
     need("g", "loc", loc)
     for sem in ("gs", "vs", "ss", "ps"):

@@ -8,9 +8,12 @@ LIST = N * LC
 ZERO = 16
 WIN = ZERO + 4 * ITEMS
 INV = 464
-ZW = 200
-NCH = 4
-OWN = 2
+SL = 8
+ZW = SL + N * CAP
+HB = CAP // 32
+NC = BAGS // 32
+RAW = N * HB + NC
+HOME = N * LC
 F32, BF, I32, U16 = "float32", "bfloat16", "int32", "uint16"
 SCRATCH = {
     "exw": ("sbuf", [128, WIN], BF),
@@ -37,16 +40,21 @@ SCRATCH = {
     "vals": ("sbuf", [128, CAP], F32),
     "inv": ("sbuf", [128, INV], F32),
     "invt": ("sbuf", [128, BAGS], F32),
+    "pm": ("sbuf", [128, NC], F32),
+    "prt": ("sbuf", [128, BAGS], F32),
+    "prw": ("sbuf", [128, INV], F32),
+    "pv": ("sbuf", [128, CAP], F32),
+    "pvt": ("sbuf", [128, CAP], F32),
     "cc": ("sbuf", [128, 16], F32),
-    "raw": ("sbuf", [32, 128], F32),
-    "offb": ("sbuf", [128, 128], U16),
+    "raw": ("sbuf", [32, 2 * RAW], F32),
+    "offb": ("sbuf", [128, 2 * RAW], U16),
     "acc": ("sbuf", [128, NB * BAGS], F32),
     "ps": ("psum", [128, 4096], F32),
 }
 for _t in range(4):
     SCRATCH["off%d" % _t] = ("sbuf", [128, 2 * LIST], U16)
-for _k in range(NCH + 1):
-    SCRATCH["z%d" % _k] = ("sbuf", [128, NB * ZW], F32)
+for _k in range(NB):
+    SCRATCH["z%d" % _k] = ("sbuf", [128, ZW], F32)
 SEMAPHORES = ["ldl", "ldx", "ldb", "ldw", "ldr", "vs", "ss", "ps", "gs", "loc", "st", "a0", "a1", "a2", "a3"]
 
 
@@ -55,9 +63,12 @@ def rank_program(g, core, T, topo):
     if r is None:
         return
     Alu, Copy = AluOpType, ActivationFunctionType.Copy
-    pair, mem = r // 2, r % 2
-    order = sorted(range(1, NCH), key=lambda x: (topo.host(T.cores[2 * x]) == topo.host(T.cores[0]), -x))
-    order.insert(OWN, 0)
+    V = g.vector
+    order = sorted(range(1, N // 2), key=lambda x: (topo.host(T.cores[2 * x]) == topo.host(T.cores[0]), -x)) + [0]
+    NCH = len(order)
+    peers = [[2 * (r // 2 ^ x) + m for m in range(2)] for x in order]
+    mem, mate = r % 2, r ^ 1
+    owners = peers[0] + peers[1] + [r] + peers[2] + [mate]
 
     cnt = {"vs": 0, "ss": 0, "ps": 0, "gs": 0}
     seen = {}
@@ -76,102 +87,151 @@ def rank_program(g, core, T, topo):
     for grp in range(2):
         g.sync.dma_start(T.lraw[16 * grp:16 * grp + 16, 0:LIST], T["it"][:, :]).then_inc(T.sem.ldl, 16)
         g.scalar.dma_start(T.lraw[16 * grp:16 * grp + 16, LIST:2 * LIST], T["it2"][:, :]).then_inc(T.sem.ldl, 16)
-    for s in range(N):
-        q = g.scalar if s % 2 else g.sync
-        q.dma_start(T.bagg[16 * s:16 * s + 16, :], T.bag[:, LC * s:LC * s + LC]).then_inc(T.sem.ldb, 16)
+    for i, s in enumerate(owners):
+        q = g.scalar if i % 2 else g.sync
+        q.dma_start(T.bagg[16 * i:16 * i + 16, :], T.bag[:, LC * s:LC * s + LC]).then_inc(T.sem.ldb, 16)
     g.sync.dma_start(T.exw[:, ZERO:WIN], T.ex[:, :]).then_inc(T.sem.ldx, 16)
     g.sync.dma_start(T.wt[:, :], T.w[:, :]).then_inc(T.sem.ldw, 16)
 
-    did("gs", g.iota(T.ip[:, :], [[1, 1]], 0, 1))
-    did("gs", g.iota(T.dumpo[:, :], [[16, LC]], BAGS + 1, 1))
-    g_io = did("gs", g.iota(T.io1[:, :], [[1, CAP]], 1, 0, allow_small_or_imprecise_dtypes=True))
-    for k in range(NCH + 1):
-        whole = k in (OWN, NCH)
-        for o in range(1 if whole else NB):
-            n = NB * ZW if whole else 1
-            g_z = did("gs", g.iota(T["z%d" % k][:, o * ZW:o * ZW + n], [[0, n]], 0, 0, allow_small_or_imprecise_dtypes=True))
-    did("vs", g.vector.memset(T.exw[:, 0:ZERO], 0.0))
-    did("vs", g.vector.memset(T.inv[:, :], 0.0))
+    def zeros(ap, n):
+        return did("gs", g.iota(ap, [[0, n]], 0, 0, allow_small_or_imprecise_dtypes=True))
+    g_ip = did("gs", g.iota(T.ip[:, :], [[1, 1]], 0, 1))
+    g_io = did("gs", g.iota(T.io1[:, :], [[1, CAP]], 0, 0, allow_small_or_imprecise_dtypes=True))
+    g_du = did("gs", g.iota(T.dumpo[:, :], [[16, LC]], BAGS + 1, 1))
+    g_pt = zeros(T.prt[:, :], BAGS)
+    g_pw = zeros(T.prw[:, BAGS:INV], INV - BAGS)
+    for o in range(NB):
+        g_z = zeros(T["z%d" % o][:, 0:SL], SL)
+    did("vs", V.memset(T.exw[:, 0:ZERO], 0.0))
+    did("vs", V.memset(T.inv[:, :], 0.0))
+    need("v", "gs", g_ip)
+    k = did("vs", V.tensor_scalar(T.ip2[:, :], T.ip[:, :], 4, None, Alu.arith_shift_right))
+    need("v", "vs", k)
+    k = did("vs", V.tensor_scalar(T.ipf[:, :], T.ip2[:, :], float(CAP), float(SL), Alu.mult, Alu.add))
     need("v", "gs", g_io)
-    k = did("vs", g.vector.tensor_scalar(T.ip2[:, :], T.ip[:, :], 4, 1, Alu.arith_shift_right, Alu.bitwise_and))
     need("v", "vs", k)
-    k = did("vs", g.vector.tensor_scalar(T.ipf[:, :], T.ip2[:, :], float(CAP), None, Alu.mult))
-    need("v", "vs", k)
-    did("vs", g.vector.tensor_scalar(T.vals[:, :], T.io1[:, :], T.ipf[:, 0:1], None, Alu.add))
+    did("vs", V.tensor_scalar(T.vals[:, :], T.io1[:, :], T.ipf[:, 0:1], None, Alu.add))
+
+    last = [0]
+    steps = []
+
+    def step(f, *waits):
+        def run():
+            for sem, val in waits:
+                need("v", sem, val)
+            need("v", "vs", last[0])
+            last[0] = did("vs", f())
+        steps.append(run)
+
+    def run_steps(n):
+        for f in steps[:n]:
+            f()
+        del steps[:n]
+
+    step(lambda: V.tensor_scalar(T.neg[:, :], T.bagg[:, :], 0, None, Alu.is_lt), ("ldb", 16 * N))
+    step(lambda: V.tensor_tensor(T.dmp[:, :], T.neg[:, :], T.dumpo[:, :], Alu.mult), ("gs", g_du))
+    step(lambda: V.tensor_tensor(T.bo[:, :], T.bagg[:, :], T.dmp[:, :], Alu.add))
+    step(lambda: V.tensor_copy(T.boff[:, :], T.bo[:, :]))
+    step(lambda: V.tensor_copy(T.inv[:, 0:INV].indirect(T.boff[:, 0:LC]), T.vals[:, :]))
+    step(lambda: V.transpose(T.invt[:, :], T.inv[:, 0:BAGS]))
+    step(lambda: V.tensor_tensor(T.pm[:, :], T.invt[:, 0:BAGS:32], T.invt[:, 16:BAGS:32], Alu.max))
+    for a in range(1, 4):
+        p, n = 32 * a - 32, 32 * a
+        step(lambda p=p, n=n: V.tensor_copy(T.prt[n:n + 32, 0:BAGS:32], T.pm[p:p + 32, :]), ("gs", g_pt))
+        to = T.pm[n:n + 32, :] if a < 3 else T.cc[n:n + 32, 2 * HB:2 * HB + NC]
+        step(lambda n=n, to=to: V.tensor_tensor(to, T.prt[n:n + 32, 0:BAGS:32], T.pm[n:n + 32, :], Alu.max))
+    step(lambda: V.tensor_tensor(T.prt[:, 16:BAGS:32], T.prt[:, 0:BAGS:32], T.invt[:, 0:BAGS:32], Alu.max))
+    step(lambda: V.transpose(T.prw[:, 0:BAGS], T.prt[:, :]))
+    step(lambda: V.tensor_copy(T.pv[:, :], T.prw[:, 0:INV].indirect(T.boff[:, 0:LC])), ("gs", g_pw))
+    step(lambda: V.transpose(T.pvt[:, :], T.pv[:, :]))
+
+    def extract():
+        need("v", "vs", last[0])
+        for hh in range(2):
+            last[0] = did("vs", V.tensor_copy(T.cc[:, HB * hh:HB * hh + HB], T.pvt[:, 16 * hh:CAP:32]))
+        need("y", "vs", last[0])
+        for a in range(4):
+            n = 2 * HB + (NC if a == 3 else 0)
+            for hh in range(2):
+                for grp in range(2):
+                    b = RAW * hh + 2 * HB * a
+                    g.sync.dma_start(T.raw[16 * grp:16 * grp + 16, b:b + n],
+                                     T.cc[32 * a + 16 * hh:32 * a + 16 * hh + 16, 0:n]).then_inc(T.sem.ldr, 16)
+
+    def spread():
+        need("v", "ldr", 16 * 16)
+        for hh in range(2):
+            last[0] = did("vs", V.tensor_copy(T.offb[0:32, hh:2 * RAW:2], T.raw[:, RAW * hh:RAW * hh + RAW]))
+
+    def spread_on():
+        need("v", "vs", last[0])
+        for qd in range(1, 4):
+            last[0] = did("vs", V.tensor_copy(T.offb[32 * qd:32 * qd + 32, :], T.offb[0:32, :]))
 
     need("v", "ldl", 64)
     for qd in range(1, 4):
-        k = did("vs", g.vector.tensor_copy(T.lraw[32 * qd:32 * qd + 32, :], T.lraw[0:32, :]))
+        k = did("vs", V.tensor_copy(T.lraw[32 * qd:32 * qd + 32, :], T.lraw[0:32, :]))
+    run_steps(1)
     need("v", "vs", k)
     v_off = []
     for t in range(4):
-        v_off.append(did("vs", g.vector.tensor_scalar(T["off%d" % t][:, :], T.lraw[:, :], 4.0, float(ZERO + t), Alu.mult, Alu.add)))
-
-    need("v", "ldb", 16 * N)
-    k = did("vs", g.vector.tensor_scalar(T.neg[:, :], T.bagg[:, :], 0, None, Alu.is_lt))
-    need("v", "vs", k)
-    k = did("vs", g.vector.tensor_tensor(T.dmp[:, :], T.neg[:, :], T.dumpo[:, :], Alu.mult))
-    need("v", "vs", k)
-    k = did("vs", g.vector.tensor_tensor(T.bo[:, :], T.bagg[:, :], T.dmp[:, :], Alu.add))
-    need("v", "vs", k)
-    k = did("vs", g.vector.tensor_copy(T.boff[:, :], T.bo[:, :]))
-    need("v", "vs", k)
-    k = did("vs", g.vector.tensor_copy(T.inv[:, 0:INV].indirect(T.boff[:, 0:LC]), T.vals[:, :]))
-    need("v", "vs", k)
-    k = did("vs", g.vector.transpose(T.invt[:, :], T.inv[:, 0:BAGS]))
-    need("v", "vs", k)
-    did("vs", g.vector.tensor_copy(T.cc[:, 0:8], T.invt[:, 0:BAGS:32]))
-    v_cc = did("vs", g.vector.tensor_copy(T.cc[:, 8:16], T.invt[:, 16:BAGS:32]))
-    need("y", "vs", v_cc)
-    for grp in range(2):
-        for a in range(4):
-            for hh in range(2):
-                g.sync.dma_start(T.raw[16 * grp:16 * grp + 16, 64 * hh + 16 * a:64 * hh + 16 * a + 16],
-                                 T.cc[32 * a + 16 * hh:32 * a + 16 * hh + 16, :]).then_inc(T.sem.ldr, 16)
+        v_off.append(did("vs", V.tensor_scalar(T["off%d" % t][:, :], T.lraw[:, :], 4.0, float(ZERO + t), Alu.mult, Alu.add)))
+        run_steps(1)
+    run_steps(4)
 
     s_u = {}
     need("s", "ldx", 16)
-    for c, x in enumerate(order):
-        l0 = 2 * LC * (pair ^ x)
+    for c in range(NCH):
+        l = LC * peers[c][0]
         for t in range(4):
             need("s", "vs", v_off[t])
             b = (4 * c + t) * PAIR
-            s_u[c, t] = did("ss", g.scalar.activation(T.hu[:, b:b + PAIR], T.exw[:, 0:WIN].indirect(T["off%d" % t][:, l0:l0 + 2 * LC]), Copy))
-    need("v", "ldx", 16)
-    v_q = []
-    for c, x in enumerate(order):
-        l0 = LIST + 2 * LC * (pair ^ x)
-        for t in range(4):
-            need("v", "vs", v_off[t])
-            need("v", "ss", s_u[c, t])
-            b = (4 * c + t) * PAIR
-            k = did("vs", g.vector.tensor_tensor(T.h[:, 4 * c * PAIR + t:4 * (c + 1) * PAIR:4],
-                                                 T.exw[:, 0:WIN].indirect(T["off%d" % t][:, l0:l0 + 2 * LC]), T.hu[:, b:b + PAIR], Alu.add))
-        need("v", "vs", k)
-        v_q.append(did("vs", g.vector.quantize_mx(T.q[:, c * PAIR:(c + 1) * PAIR], T.qsc[:, c * PAIR:(c + 1) * PAIR],
-                                                  T.h[:, 4 * c * PAIR:4 * (c + 1) * PAIR])))
-        if c == OWN - 1:
-            need("v", "ldw", 16)
-            v_w = did("vs", g.vector.quantize_mx(T.wq[:, :], T.wsc[:, :], T.wt[:, :]))
-        if c == OWN:
-            need("v", "ldr", 16 * 16)
-            for hh in range(2):
-                k = did("vs", g.vector.tensor_copy(T.offb[0:32, hh:128:2], T.raw[:, 64 * hh:64 * hh + 64]))
-            need("v", "vs", k)
-            for qd in range(1, 4):
-                v_ob = did("vs", g.vector.tensor_copy(T.offb[32 * qd:32 * qd + 32, :], T.offb[0:32, :]))
+            s_u[c, t] = did("ss", g.scalar.activation(T.hu[:, b:b + PAIR], T.exw[:, 0:WIN].indirect(T["off%d" % t][:, l:l + 2 * LC]), Copy))
+    v_h = [0] * NCH
+    v_q = [0] * NCH
 
-    def land(c, rx_mem, tx_mem):
-        if c == 1:
-            return PAIR + CAP * tx_mem + (0 if rx_mem == 0 else CAP)
-        if c == OWN:
-            return PAIR + (PAIR if rx_mem == 0 else 0)
-        return (0 if c == 0 else PAIR + PAIR + CAP) + CAP * tx_mem
+    def part(c, t):
+        need("v", "ldx", 16)
+        need("v", "vs", v_off[t])
+        need("v", "ss", s_u[c, t])
+        b = (4 * c + t) * PAIR
+        l = LIST + LC * peers[c][0]
+        v_h[c] = did("vs", V.tensor_tensor(T.h[:, 4 * c * PAIR + t:4 * (c + 1) * PAIR:4],
+                                           T.exw[:, 0:WIN].indirect(T["off%d" % t][:, l:l + 2 * LC]), T.hu[:, b:b + PAIR], Alu.add))
+
+    def quant(c):
+        need("v", "vs", v_h[c])
+        a, b = c * PAIR, (c + 1) * PAIR
+        v_q[c] = did("vs", V.quantize_mx(T.q[:, a:b], T.qsc[:, a:b], T.h[:, 4 * a:4 * b]))
+
+    for t in range(4):
+        part(0, t)
+        run_steps(1)
+    run_steps(1)
+    quant(0)
+    for t in range(3):
+        part(1, t)
+        run_steps(1)
+    part(1, 3)
+    extract()
+    part(2, 0)
+    quant(1)
+    for t in range(1, 4):
+        part(2, t)
+    part(3, 0)
+    quant(2)
+    need("v", "ldw", 16)
+    v_w = did("vs", V.quantize_mx(T.wq[:, :], T.wsc[:, :], T.wt[:, :]))
+    for t in range(1, 4):
+        part(3, t)
+    spread()
+    quant(3)
+    spread_on()
 
     loc = 0
     arr = []
-    for c, x in enumerate(order):
-        dests = [2 * (pair ^ x) + m for m in range(2) if 2 * (pair ^ x) + m != r]
+    for c in range(NCH):
+        dests = [d for d in peers[c] if d != r]
         need("g", "vs", v_q[c])
         for kind in range(2):
             tr, tot = [], 0
@@ -181,7 +241,7 @@ def rank_program(g, core, T, topo):
                 n = len(eng) // len(dests)
                 rid, pnc = topo.addr(dst, core)
                 a = c * PAIR + CAP * (d % 2)
-                b = land(c, d % 2, mem)
+                b = c * PAIR + (CAP * mem if c < NCH - 1 else 0)
                 if kind == 0:
                     src, out = T.q[:, a:a + CAP].bitcast(dt.uint8), T.lq[:, b:b + CAP].bitcast(dt.uint8)
                 else:
@@ -193,58 +253,59 @@ def rank_program(g, core, T, topo):
             loc += tot
         arr.append(2 * tot)
 
-    need("s", "gs", g_z)
     need("t", "vs", v_w)
     use = 0
     bank_free = [0] * 8
-    a_v, s_base = [0] * NB, [0] * NB
-    own_win, z_own = [], []
-    for stage in (NCH, 0, 1, OWN, NCH - 1):
-        z = T["z%d" % stage]
-        src, ssc = T.lq, T.lsc
-        lo, width = 0, PAIR
-        if stage == NCH:
-            first = OWN * PAIR
-            owners, src, ssc, lo, width = [r], T.q, T.qsc, CAP * mem, CAP
-            need("t", "vs", v_q[OWN])
-        elif stage == OWN:
-            owners = [r ^ 1]
-            lo, width = CAP * (1 - mem), CAP
-            first = land(OWN, mem, 1 - mem) - lo
-        else:
-            owners = [2 * (pair ^ order[stage]) + m for m in range(2)]
-            first = land(stage, mem, 0)
-        if stage < NCH:
-            need("t", "a%d" % stage, arr[stage])
-        zs = []
+    z_in = {}
+    own = (NCH - 1) * PAIR + CAP * mem
+    own_first = min(own, N * CAP - 128)
+    mate_first = (NCH - 1) * PAIR + CAP - 128
+    stages = [(T.lq, T.lsc, 0, 0, PAIR, 0, "a0", arr[0]),
+              (T.lq, T.lsc, PAIR, 0, PAIR, 2, "a1", arr[1]),
+              (T.q, T.qsc, own_first, own - own_first, CAP, 4, "vs", v_q[3]),
+              (T.lq, T.lsc, 2 * PAIR, 0, PAIR, 5, "a2", arr[2]),
+              (T.lq, T.lsc, mate_first, 128 - CAP, CAP, 7, "a3", arr[3])]
+    for src, ssc, first, lo, width, place, sem, val in stages:
+        need("t", sem, val)
+        n = max(128, width)
         for o in range(NB):
             bk = use % 8
             use += 1
             need("t", "ss", bank_free[bk])
-            p = did("ps", g.tensor.matmul_mx(T.ps[:, 512 * bk:512 * bk + PAIR], T.wq[:, 128 * o:128 * o + 128], T.wsc[:, 128 * o:128 * o + 128],
-                                             src[:, first:first + PAIR], ssc[:, first:first + PAIR], True, True))
-            if stage == 0:
-                need("s", "vs", v_ob)
-                need("s", "ss", z_own[o])
-                s_base[o] = did("ss", g.scalar.activation(T.acc[:, BAGS * o:BAGS * (o + 1)], own_win[o], Copy))
+            p = did("ps", g.tensor.matmul_mx(T.ps[:, 512 * bk:512 * bk + n], T.wq[:, 128 * o:128 * o + 128], T.wsc[:, 128 * o:128 * o + 128],
+                                             src[:, first:first + n], ssc[:, first:first + n], True, True))
             need("s", "ps", p)
-            zs.append(did("ss", g.scalar.activation(z[:, o * ZW + 1 + lo:o * ZW + 1 + lo + width],
-                                                    T.ps[:, 512 * bk + lo:512 * bk + lo + width], Copy)))
-            bank_free[bk] = zs[o]
-        last = stage == NCH - 1
-        for s, o in [(s, o) for o in range(NB) for s in owners] if last else [(s, o) for s in owners for o in range(NB)]:
-            y = T.acc[:, BAGS * o:BAGS * (o + 1)]
-            win = z[:, o * ZW:o * ZW + 1 + lo + width].indirect(T.offb[:, 16 * s:16 * s + 16])
-            if stage == NCH:
-                own_win.append(win)
-                z_own.append(zs[o])
-                continue
-            need("v", "ss", max(zs[o], s_base[o]))
-            need("v", "vs", a_v[o])
-            a_v[o] = did("vs", g.vector.tensor_tensor(y, win, y, Alu.add))
-            if last and s == owners[-1]:
-                need("y", "vs", a_v[o])
-                g.sync.dma_start(T.y[:, BAGS * o:BAGS * (o + 1)], y).then_inc(T.sem.st, 16)
+            b = SL + CAP * place
+            k = did("ss", g.scalar.activation(T["z%d" % o][:, b:b + width], T.ps[:, 512 * bk + lo:512 * bk + lo + width], Copy))
+            bank_free[bk] = k
+            for i in range(width // CAP):
+                z_in[place + i, o] = k
+
+    chain = [0] * NB
+    for i in range(1, N):
+        for o in (0, 2, 1) if i == N - 1 else range(NB):
+            z = T["z%d" % o]
+            b = SL + CAP * i
+            need("v", "gs", g_z)
+            need("v", "vs", max(chain[o], last[0]))
+            need("v", "ss", z_in[i, o])
+            chain[o] = did("vs", V.tensor_tensor(z[:, b:b + CAP], z[:, 0:b].indirect(T.offb[:, LC * i:LC * i + LC]), z[:, b:b + CAP], Alu.add))
+
+    for o in (0, 2, 1):
+        y = T.acc[:, BAGS * o:BAGS * (o + 1)]
+        win = T["z%d" % o][:, 0:ZW].indirect(T.offb[:, HOME:HOME + BAGS // 16])
+        if o == 2:
+            need("v", "vs", chain[o])
+            k = did("vs", V.tensor_copy(y, win))
+            need("y", "vs", k)
+            q = g.sync
+        else:
+            need("s", "gs", g_z)
+            need("s", "vs", chain[o])
+            k = did("ss", g.scalar.activation(y, win, Copy))
+            q = g.scalar if o == 1 else g.sync
+            need("s" if o == 1 else "y", "ss", k)
+        q.dma_start(T.y[:, BAGS * o:BAGS * (o + 1)], y).then_inc(T.sem.st, 16)
 
     need("g", "loc", loc)
     for sem in ("gs", "vs", "ss", "ps"):

from concourse.bass import DstId, RemoteDMATransfer
from concourse.mybir import dt, AluOpType, ActivationFunctionType

N, CAP, BAGS, NB, ITEMS = 8, 96, 256, 3, 512
PAIR = 2 * CAP
LC = CAP // 16
LIST = N * LC
ZERO = 16
WIN = ZERO + 4 * ITEMS
INV = 464
SL = 8
ZW = SL + N * CAP
HB = CAP // 32
NC = BAGS // 32
RAW = N * HB + NC
HOME = N * LC
F32, BF, I32, U16 = "float32", "bfloat16", "int32", "uint16"
SCRATCH = {
    "exw": ("sbuf", [128, WIN], BF),
    "wt": ("sbuf", [128, 512 * NB], BF),
    "wq": ("sbuf", [128, 128 * NB], "float8_e4m3fn_x4"),
    "wsc": ("sbuf", [128, 128 * NB], "uint8"),
    "lraw": ("sbuf", [128, 2 * LIST], I32),
    "hu": ("sbuf", [128, 4 * N * CAP], BF),
    "h": ("sbuf", [128, 4 * N * CAP], BF),
    "q": ("sbuf", [128, N * CAP], "float8_e4m3fn_x4"),
    "qsc": ("sbuf", [128, N * CAP], "uint8"),
    "lq": ("sbuf", [128, N * CAP], "float8_e4m3fn_x4"),
    "lsc": ("sbuf", [128, N * CAP], "uint8"),
    "bagg": ("sbuf", [128, LC], I32),
    "neg": ("sbuf", [128, LC], I32),
    "dumpo": ("sbuf", [128, LC], I32),
    "dmp": ("sbuf", [128, LC], I32),
    "bo": ("sbuf", [128, LC], I32),
    "boff": ("sbuf", [128, LC], U16),
    "ip": ("sbuf", [128, 1], I32),
    "ip2": ("sbuf", [128, 1], I32),
    "ipf": ("sbuf", [128, 1], F32),
    "io1": ("sbuf", [128, CAP], F32),
    "vals": ("sbuf", [128, CAP], F32),
    "inv": ("sbuf", [128, INV], F32),
    "invt": ("sbuf", [128, BAGS], F32),
    "pm": ("sbuf", [128, NC], F32),
    "prt": ("sbuf", [128, BAGS], F32),
    "prw": ("sbuf", [128, INV], F32),
    "pv": ("sbuf", [128, CAP], F32),
    "pvt": ("sbuf", [128, CAP], F32),
    "cc": ("sbuf", [128, 16], F32),
    "raw": ("sbuf", [32, 2 * RAW], F32),
    "offb": ("sbuf", [128, 2 * RAW], U16),
    "acc": ("sbuf", [128, NB * BAGS], F32),
    "ps": ("psum", [128, 4096], F32),
}
for _t in range(4):
    SCRATCH["off%d" % _t] = ("sbuf", [128, 2 * LIST], U16)
for _k in range(NB):
    SCRATCH["z%d" % _k] = ("sbuf", [128, ZW], F32)
SEMAPHORES = ["ldl", "ldx", "ldb", "ldw", "ldr", "vs", "ss", "ps", "gs", "loc", "st", "a0", "a1", "a2", "a3"]


def rank_program(g, core, T, topo):
    r = T.rank_of(core)
    if r is None:
        return
    Alu, Copy = AluOpType, ActivationFunctionType.Copy
    V = g.vector
    order = sorted(range(1, N // 2), key=lambda x: (topo.host(T.cores[2 * x]) == topo.host(T.cores[0]), -x)) + [0]
    NCH = len(order)
    peers = [[2 * (r // 2 ^ x) + m for m in range(2)] for x in order]
    mem, mate = r % 2, r ^ 1
    owners = peers[0] + peers[1] + [r] + peers[2] + [mate]

    cnt = {"vs": 0, "ss": 0, "ps": 0, "gs": 0}
    seen = {}
    queues = {"v": g.vector, "s": g.scalar, "t": g.tensor, "y": g.sync, "g": g}

    def need(qn, sem, val):
        if val > seen.get((qn, sem), 0):
            queues[qn].wait_ge(T.sem[sem], val)
            seen[(qn, sem)] = val

    def did(sem, ins):
        ins.then_inc(T.sem[sem], 1)
        cnt[sem] += 1
        return cnt[sem]

    for grp in range(2):
        g.sync.dma_start(T.lraw[16 * grp:16 * grp + 16, 0:LIST], T["it"][:, :]).then_inc(T.sem.ldl, 16)
        g.scalar.dma_start(T.lraw[16 * grp:16 * grp + 16, LIST:2 * LIST], T["it2"][:, :]).then_inc(T.sem.ldl, 16)
    for i, s in enumerate(owners):
        q = g.scalar if i % 2 else g.sync
        q.dma_start(T.bagg[16 * i:16 * i + 16, :], T.bag[:, LC * s:LC * s + LC]).then_inc(T.sem.ldb, 16)
    g.sync.dma_start(T.exw[:, ZERO:WIN], T.ex[:, :]).then_inc(T.sem.ldx, 16)
    g.sync.dma_start(T.wt[:, :], T.w[:, :]).then_inc(T.sem.ldw, 16)

    def zeros(ap, n):
        return did("gs", g.iota(ap, [[0, n]], 0, 0, allow_small_or_imprecise_dtypes=True))
    g_ip = did("gs", g.iota(T.ip[:, :], [[1, 1]], 0, 1))
    g_io = did("gs", g.iota(T.io1[:, :], [[1, CAP]], 0, 0, allow_small_or_imprecise_dtypes=True))
    g_du = did("gs", g.iota(T.dumpo[:, :], [[16, LC]], BAGS + 1, 1))
    g_pt = zeros(T.prt[:, :], BAGS)
    g_pw = zeros(T.prw[:, BAGS:INV], INV - BAGS)
    for o in range(NB):
        g_z = zeros(T["z%d" % o][:, 0:SL], SL)
    did("vs", V.memset(T.exw[:, 0:ZERO], 0.0))
    did("vs", V.memset(T.inv[:, :], 0.0))
    need("v", "gs", g_ip)
    k = did("vs", V.tensor_scalar(T.ip2[:, :], T.ip[:, :], 4, None, Alu.arith_shift_right))
    need("v", "vs", k)
    k = did("vs", V.tensor_scalar(T.ipf[:, :], T.ip2[:, :], float(CAP), float(SL), Alu.mult, Alu.add))
    need("v", "gs", g_io)
    need("v", "vs", k)
    did("vs", V.tensor_scalar(T.vals[:, :], T.io1[:, :], T.ipf[:, 0:1], None, Alu.add))

    last = [0]
    steps = []

    def step(f, *waits):
        def run():
            for sem, val in waits:
                need("v", sem, val)
            need("v", "vs", last[0])
            last[0] = did("vs", f())
        steps.append(run)

    def run_steps(n):
        for f in steps[:n]:
            f()
        del steps[:n]

    step(lambda: V.tensor_scalar(T.neg[:, :], T.bagg[:, :], 0, None, Alu.is_lt), ("ldb", 16 * N))
    step(lambda: V.tensor_tensor(T.dmp[:, :], T.neg[:, :], T.dumpo[:, :], Alu.mult), ("gs", g_du))
    step(lambda: V.tensor_tensor(T.bo[:, :], T.bagg[:, :], T.dmp[:, :], Alu.add))
    step(lambda: V.tensor_copy(T.boff[:, :], T.bo[:, :]))
    step(lambda: V.tensor_copy(T.inv[:, 0:INV].indirect(T.boff[:, 0:LC]), T.vals[:, :]))
    step(lambda: V.transpose(T.invt[:, :], T.inv[:, 0:BAGS]))
    step(lambda: V.tensor_tensor(T.pm[:, :], T.invt[:, 0:BAGS:32], T.invt[:, 16:BAGS:32], Alu.max))
    for a in range(1, 4):
        p, n = 32 * a - 32, 32 * a
        step(lambda p=p, n=n: V.tensor_copy(T.prt[n:n + 32, 0:BAGS:32], T.pm[p:p + 32, :]), ("gs", g_pt))
        to = T.pm[n:n + 32, :] if a < 3 else T.cc[n:n + 32, 2 * HB:2 * HB + NC]
        step(lambda n=n, to=to: V.tensor_tensor(to, T.prt[n:n + 32, 0:BAGS:32], T.pm[n:n + 32, :], Alu.max))
    step(lambda: V.tensor_tensor(T.prt[:, 16:BAGS:32], T.prt[:, 0:BAGS:32], T.invt[:, 0:BAGS:32], Alu.max))
    step(lambda: V.transpose(T.prw[:, 0:BAGS], T.prt[:, :]))
    step(lambda: V.tensor_copy(T.pv[:, :], T.prw[:, 0:INV].indirect(T.boff[:, 0:LC])), ("gs", g_pw))
    step(lambda: V.transpose(T.pvt[:, :], T.pv[:, :]))

    def extract():
        need("v", "vs", last[0])
        for hh in range(2):
            last[0] = did("vs", V.tensor_copy(T.cc[:, HB * hh:HB * hh + HB], T.pvt[:, 16 * hh:CAP:32]))
        need("y", "vs", last[0])
        for a in range(4):
            n = 2 * HB + (NC if a == 3 else 0)
            for hh in range(2):
                for grp in range(2):
                    b = RAW * hh + 2 * HB * a
                    g.sync.dma_start(T.raw[16 * grp:16 * grp + 16, b:b + n],
                                     T.cc[32 * a + 16 * hh:32 * a + 16 * hh + 16, 0:n]).then_inc(T.sem.ldr, 16)

    def spread():
        need("v", "ldr", 16 * 16)
        for hh in range(2):
            last[0] = did("vs", V.tensor_copy(T.offb[0:32, hh:2 * RAW:2], T.raw[:, RAW * hh:RAW * hh + RAW]))

    def spread_on():
        need("v", "vs", last[0])
        for qd in range(1, 4):
            last[0] = did("vs", V.tensor_copy(T.offb[32 * qd:32 * qd + 32, :], T.offb[0:32, :]))

    need("v", "ldl", 64)
    for qd in range(1, 4):
        k = did("vs", V.tensor_copy(T.lraw[32 * qd:32 * qd + 32, :], T.lraw[0:32, :]))
    run_steps(1)
    need("v", "vs", k)
    v_off = []
    for t in range(4):
        v_off.append(did("vs", V.tensor_scalar(T["off%d" % t][:, :], T.lraw[:, :], 4.0, float(ZERO + t), Alu.mult, Alu.add)))
        run_steps(1)
    run_steps(4)

    s_u = {}
    need("s", "ldx", 16)
    for c in range(NCH):
        l = LC * peers[c][0]
        for t in range(4):
            need("s", "vs", v_off[t])
            b = (4 * c + t) * PAIR
            s_u[c, t] = did("ss", g.scalar.activation(T.hu[:, b:b + PAIR], T.exw[:, 0:WIN].indirect(T["off%d" % t][:, l:l + 2 * LC]), Copy))
    v_h = [0] * NCH
    v_q = [0] * NCH

    def part(c, t):
        need("v", "ldx", 16)
        need("v", "vs", v_off[t])
        need("v", "ss", s_u[c, t])
        b = (4 * c + t) * PAIR
        l = LIST + LC * peers[c][0]
        v_h[c] = did("vs", V.tensor_tensor(T.h[:, 4 * c * PAIR + t:4 * (c + 1) * PAIR:4],
                                           T.exw[:, 0:WIN].indirect(T["off%d" % t][:, l:l + 2 * LC]), T.hu[:, b:b + PAIR], Alu.add))

    def quant(c):
        need("v", "vs", v_h[c])
        a, b = c * PAIR, (c + 1) * PAIR
        v_q[c] = did("vs", V.quantize_mx(T.q[:, a:b], T.qsc[:, a:b], T.h[:, 4 * a:4 * b]))

    for t in range(4):
        part(0, t)
        run_steps(1)
    run_steps(1)
    quant(0)
    for t in range(3):
        part(1, t)
        run_steps(1)
    part(1, 3)
    extract()
    part(2, 0)
    quant(1)
    for t in range(1, 4):
        part(2, t)
    part(3, 0)
    quant(2)
    need("v", "ldw", 16)
    v_w = did("vs", V.quantize_mx(T.wq[:, :], T.wsc[:, :], T.wt[:, :]))
    for t in range(1, 4):
        part(3, t)
    spread()
    quant(3)
    spread_on()

    loc = 0
    arr = []
    for c in range(NCH):
        dests = [d for d in peers[c] if d != r]
        need("g", "vs", v_q[c])
        for kind in range(2):
            tr, tot = [], 0
            for i, d in enumerate(dests):
                dst = T.cores[d]
                eng = topo.engines(core, dst)
                n = len(eng) // len(dests)
                rid, pnc = topo.addr(dst, core)
                a = c * PAIR + CAP * (d % 2)
                b = c * PAIR + (CAP * mem if c < NCH - 1 else 0)
                if kind == 0:
                    src, out = T.q[:, a:a + CAP].bitcast(dt.uint8), T.lq[:, b:b + CAP].bitcast(dt.uint8)
                else:
                    src, out = T.qsc[:, a:a + CAP], T.lsc[:, b:b + CAP]
                tr.append(RemoteDMATransfer(dst_ids=[DstId(rid=rid, pnc=pnc)], dma_engine_mask=sum(1 << e for e in eng[i * n:(i + 1) * n]),
                                            remote_sem=T.sem["a%d" % c], src=src, dst=out))
                tot += n
            g.remote_dma_fused(tr, local_sem=T.sem.loc)
            loc += tot
        arr.append(2 * tot)

    need("t", "vs", v_w)
    use = 0
    bank_free = [0] * 8
    z_in = {}
    own = (NCH - 1) * PAIR + CAP * mem
    own_first = min(own, N * CAP - 128)
    mate_first = (NCH - 1) * PAIR + CAP - 128
    stages = [(T.lq, T.lsc, 0, 0, PAIR, 0, "a0", arr[0]),
              (T.lq, T.lsc, PAIR, 0, PAIR, 2, "a1", arr[1]),
              (T.q, T.qsc, own_first, own - own_first, CAP, 4, "vs", v_q[3]),
              (T.lq, T.lsc, 2 * PAIR, 0, PAIR, 5, "a2", arr[2]),
              (T.lq, T.lsc, mate_first, 128 - CAP, CAP, 7, "a3", arr[3])]
    for src, ssc, first, lo, width, place, sem, val in stages:
        need("t", sem, val)
        n = max(128, width)
        for o in range(NB):
            bk = use % 8
            use += 1
            need("t", "ss", bank_free[bk])
            p = did("ps", g.tensor.matmul_mx(T.ps[:, 512 * bk:512 * bk + n], T.wq[:, 128 * o:128 * o + 128], T.wsc[:, 128 * o:128 * o + 128],
                                             src[:, first:first + n], ssc[:, first:first + n], True, True))
            need("s", "ps", p)
            b = SL + CAP * place
            k = did("ss", g.scalar.activation(T["z%d" % o][:, b:b + width], T.ps[:, 512 * bk + lo:512 * bk + lo + width], Copy))
            bank_free[bk] = k
            for i in range(width // CAP):
                z_in[place + i, o] = k

    chain = [0] * NB
    for i in range(1, N):
        for o in (0, 2, 1) if i == N - 1 else range(NB):
            z = T["z%d" % o]
            b = SL + CAP * i
            need("v", "gs", g_z)
            need("v", "vs", max(chain[o], last[0]))
            need("v", "ss", z_in[i, o])
            chain[o] = did("vs", V.tensor_tensor(z[:, b:b + CAP], z[:, 0:b].indirect(T.offb[:, LC * i:LC * i + LC]), z[:, b:b + CAP], Alu.add))

    for o in (0, 2, 1):
        y = T.acc[:, BAGS * o:BAGS * (o + 1)]
        win = T["z%d" % o][:, 0:ZW].indirect(T.offb[:, HOME:HOME + BAGS // 16])
        if o == 2:
            need("v", "vs", chain[o])
            k = did("vs", V.tensor_copy(y, win))
            need("y", "vs", k)
            q = g.sync
        else:
            need("s", "gs", g_z)
            need("s", "vs", chain[o])
            k = did("ss", g.scalar.activation(y, win, Copy))
            q = g.scalar if o == 1 else g.sync
            need("s" if o == 1 else "y", "ss", k)
        q.dma_start(T.y[:, BAGS * o:BAGS * (o + 1)], y).then_inc(T.sem.st, 16)

    need("g", "loc", loc)
    for sem in ("gs", "vs", "ss", "ps"):
        need("g", sem, cnt[sem])
    need("g", "st", 16 * NB)
